import numpy as np, ml_dtypes
CORES = [4,20,36,52,68,84,100,116,12,28,44,60,76,92,108,124]
N = 16
PERM = [[0,8],[1,9],[2,10],[3,11],[4,12],[5,13],[6,14],[7,15],[8,0],[9,1],[10,2],[11,3],[12,4],[13,5],[14,6],[15,7]]
def setup_inputs(rng):
    return {"x": rng.standard_normal((N, 128, 8), dtype=np.float32).astype(ml_dtypes.bfloat16)}
def reference(x):
    y = np.empty_like(x)
    for s, d in PERM:
        y[d] = x[s]
    return {"y": y}

SCRATCH = {
    "stage": ("dram", [128, 8], "bfloat16"),
    "relay": ("dram", [128, 8], "bfloat16"),
    "land": ("dram", [128, 8], "bfloat16"),
}
SEMAPHORES = ["loaded", "sent", "relayed", "arrived", "stored"]

ENGINES = 4
MASK = 0x000F


def _helper(topo, group, src, dst):
    if topo.may_write(src, dst):
        return None
    base = topo.chip(src) * 8
    for h in range(base, base + 8):
        if h not in group and topo.die(h) == topo.die(src) and topo.may_write(h, dst):
            return h
    return None


def rank_program(g, core, T, topo):
    group = list(T.cores)
    routes = []
    for s, d in T.tables["PERM"]:
        routes.append((group[s], _helper(topo, group, group[s], group[d]), group[d]))

    def send(out_ap, in_ap, dst, remote_sem):
        rid, pid, _se = topo.addr(dst)
        g.remote_dma(out_ap, in_ap, remote_sem, T.sem.sent, pid, rid, MASK)

    for src, via, dst in routes:
        if core == via:
            g.wait_ge(T.sem.relayed, ENGINES)
            send(T.land[:], T.relay[:], dst, T.sem.arrived)
            g.wait_ge(T.sem.sent, ENGINES)

    for src, via, dst in routes:
        if core == src:
            g.sync.dma_start(T.stage[:], T.x[:]).then_inc(T.sem.loaded, 16)
            g.wait_ge(T.sem.loaded, 16)
            if via is None:
                send(T.land[:], T.stage[:], dst, T.sem.arrived)
            else:
                send(T.relay[:], T.stage[:], via, T.sem.relayed)
            g.wait_ge(T.sem.sent, ENGINES)

    for src, via, dst in routes:
        if core == dst:
            g.sync.wait_ge(T.sem.arrived, ENGINES)
            g.sync.dma_start(T.y[:], T.land[:]).then_inc(T.sem.stored, 16)
            g.sync.wait_ge(T.sem.stored, 16)
